import numpy as np
import ml_dtypes


def mxq(x, axis, fmt="e4m3"):
    dtype, down = {"e4m3": (ml_dtypes.float8_e4m3fn, 7), "e5m2": (ml_dtypes.float8_e5m2, 14)}[fmt]
    v = np.moveaxis(np.asarray(x, np.float32).astype(ml_dtypes.bfloat16).astype(np.float64), axis, -1)
    blocks = v.reshape(v.shape[:-1] + (-1, 32))
    amax = np.abs(blocks).max(-1, keepdims=True)
    byte = np.maximum(np.where(amax > 0, np.frexp(amax)[1] - 1 + 127, 0) - down, 1)
    scale = np.exp2(byte - 127.0)
    codes = (blocks / scale).astype(np.float32).astype(dtype).astype(np.float64)
    return np.moveaxis((codes * scale).reshape(v.shape), -1, axis)


WIDE = False


def mx_kscale(k):
    if not WIDE:
        return np.ones(k)
    levels = np.array([10, -10, 5, -5, 0])
    if k % 512:
        return np.exp2(np.random.permutation(np.resize(levels, k // 32))).repeat(32)
    a = np.empty((k // 512, 16))
    for p in range(k // 512):
        a[p, :8] = np.random.permutation(np.resize(levels, 8))
        for g in range(8):
            far = levels[np.abs(levels - a[p, g]) >= 10]
            a[p, g + 8] = far[np.random.randint(len(far))]
    return np.exp2(a.ravel()).repeat(32)


def f64(x):
    return np.asarray(x).astype(np.float64)


def striped(idx):
    return np.tile(idx.reshape(-1, 16).T, (8, 1)).astype(np.uint16)


def unstriped(offs):
    return offs[:16].T.reshape(-1).astype(np.int64)


E2M1 = np.array([0.0, 0.5, 1.0, 1.5, 2.0, 3.0, 4.0, 6.0, -0.0, -0.5, -1.0, -1.5, -2.0, -3.0, -4.0, -6.0])


def pack_fp4(w):
    k, n = w.shape
    w = f64(np.asarray(w, np.float32).astype(ml_dtypes.bfloat16)).reshape(k // 32, 32, n)
    amax = np.abs(w).max(1)
    mant, ex = np.frexp(amax / 6.0)
    byte = np.clip(np.where(amax > 0, np.where(mant > 0.5, ex, ex - 1) + 127, 1), 1, 254)
    scaled = (w * np.exp2(127.0 - byte)[:, None, :]).reshape(k, n).astype(np.float32)
    c = np.ascontiguousarray(scaled.reshape(k // 512, 128, 4, n).transpose(0, 1, 3, 2)).astype(ml_dtypes.float4_e2m1fn).view(np.uint8) & 0xF
    words = (c[..., 0::2] | (c[..., 1::2] << 4)).reshape(k // 512, 128, 2 * n)
    return np.ascontiguousarray(words), np.ascontiguousarray(byte.astype(np.uint8).reshape(k // 512, 16, n))


def unpack_fp4(words, scales):
    g, _, n = scales.shape
    words = np.ascontiguousarray(words).reshape(g, 128, n, 2)
    nib = np.empty((g, 128, n, 4), np.uint8)
    nib[..., 0::2] = words & 0xF
    nib[..., 1::2] = words >> 4
    vals = E2M1[nib] * np.repeat(np.exp2(scales.astype(np.float64) - 127.0), 8, axis=1)[..., None]
    return vals.transpose(0, 1, 3, 2).reshape(g * 512, n)


def gelu(v):
    return 0.5 * v * (1.0 + np.tanh(np.sqrt(2.0 / np.pi) * (v + 0.044715 * v**3)))


K, T, S, V, H, N = 512, 2048, 768, 256, 512, 128


def setup_inputs():
    n = np.random.standard_normal
    s = mx_kscale(K)[:, None]
    u = mx_kscale(H)
    packed_xT = pack_fp4(n((K, T)) * s)
    return {
        "x_words": packed_xT[0],
        "x_scales": packed_xT[1],
        "w1": (n((K, H)) / np.sqrt(K) / s * u).astype(np.float32),
        "w2": (n((H, N)) / np.sqrt(2 * H) / u[:, None]).astype(np.float32),
        "w3": (n((H, N)) / np.sqrt(2 * H) / u[:, None]).astype(np.float32),
        "offs": striped(np.random.permutation(T)[:S]),
    }


def reference(x_words, x_scales, w1, w2, w3, offs):
    xq = unpack_fp4(x_words, x_scales)[:, unstriped(offs)]
    h = gelu(mxq(f64(w1), 0, "e4m3").T @ xq)
    mean = (h[:, :V] + h[:, V:2 * V] + h[:, 2 * V:3 * V]) / 3
    dev = np.sqrt(((h[:, :V] - mean) ** 2 + (h[:, V:2 * V] - mean) ** 2 + (h[:, 2 * V:3 * V] - mean) ** 2) / 3)
    return mxq(f64(w2), 0, "e4m3").T @ mxq(mean, 0, "e4m3") + mxq(f64(w3), 0, "e4m3").T @ mxq(dev, 0, "e4m3")

@@ -1,0 +1,221 @@
+import math
+from contextlib import ExitStack
+
+import concourse.mybir as mybir
+
+K, T, S, V, H, N = 512, 2048, 768, 256, 512, 128
+FLOPS = 2 * K * H * S + 2 * 2 * H * N * V
+
+F32 = mybir.dt.float32
+BF16 = mybir.dt.bfloat16
+I32 = mybir.dt.int32
+U32 = mybir.dt.uint32
+U16 = mybir.dt.uint16
+U8 = mybir.dt.uint8
+FP8X4 = mybir.dt.float8_e4m3fn_x4
+FP4X4 = mybir.dt.float4_e2m1fn_x4
+ACT = mybir.ActivationFunctionType
+ALU = mybir.AluOpType
+
+P = 128
+PACK = 4
+PIECES = 3
+SEG = 128
+CHUNKS = V // SEG
+WIDE = SEG * PACK
+W1_CUTS = ((0, 128), (128, 256), (256, 384), (384, 512))
+W1_AHEAD = 2
+SQRT_FLOOR = 2.0 ** -110
+
+
+def tile_picked_statpool_gelu_p_kernel(tc, x_words, x_scales, w1, w2, w3, offs, out):
+    nc = tc.nc
+    with ExitStack() as ctx:
+        sb = ctx.enter_context(tc.tile_pool(name="sb", bufs=1))
+        ps = ctx.enter_context(tc.psum_pool(name="ps", bufs=1))
+
+        def tile(shape, dtype, name, tag=""):
+            return sb.tile(shape, dtype, name=name, tag=tag, align_bytes=64)
+
+        offsets = sb.tile([P, S // 16], U16, name="offsets")
+        nc.sync.dma_start(offsets[:], offs)
+
+        scale_table = tile([P, T], U8, "scale_table")
+        nc.vector.memset(scale_table[:].bitcast(I32), 0)
+
+        zero_in = tile([P, 1], F32, "zero_in")
+        zero = tile([P, 1], F32, "zero")
+        nc.gpsimd.memset(zero_in[:], 0.0)
+        nc.scalar.activation(zero[:], zero_in[:], ACT.Gelu_apprx_tanh)
+
+        w1_rows = w1.rearrange("(p j) c -> p j c", j=PACK)
+        w1_raw = [tile([P, PACK, hi - lo], F32, f"w1_raw{u}") for u, (lo, hi) in enumerate(W1_CUTS)]
+
+        def load_w1(u):
+            lo, hi = W1_CUTS[u]
+            nc.sync.dma_start(w1_raw[u][:], w1_rows[:, :, lo:hi])
+
+        for u in range(W1_AHEAD):
+            load_w1(u)
+        for r in range(4):
+            nc.sync.dma_start(scale_table[r:P:32, :].bitcast(I32), x_scales[0, r:16:4, :].bitcast(I32))
+        for u in range(W1_AHEAD, len(W1_CUTS)):
+            load_w1(u)
+        word_table = tile([P, T], U16, "word_table")
+        nc.sync.dma_start(word_table[:].bitcast(I32), x_words[0].bitcast(I32))
+        w23_raw = [tile([P, PACK, N], F32, f"w23_raw{u}") for u in range(2)]
+        for u, w in enumerate((w2, w3)):
+            nc.sync.dma_start(w23_raw[u][:], w.rearrange("(p j) n -> p j n", j=PACK))
+
+        picked_scales = tile([P, S], U8, "picked_scales")
+        nc.vector.tensor_copy(picked_scales[:], scale_table[:].indirect(offsets[:]))
+
+        w1_bf = tile([P, PACK, P, PACK], BF16, "w1_bf")
+        for u, (lo, hi) in enumerate(W1_CUTS):
+            nc.scalar.activation(
+                w1_bf[:, :, lo // PACK : hi // PACK, :].rearrange("p t m j -> p m j t"),
+                w1_raw[u][:].rearrange("p j (m t) -> p m j t", t=PACK),
+                ACT.Identity,
+                bias=zero[:],
+            )
+        w1_codes = tile([P, H], U32, "w1_codes")
+        w1_scales = tile([P, H], U8, "w1_scales")
+        nc.vector.quantize_mx(
+            out=w1_codes[:].bitcast(FP8X4), scales=w1_scales[:], in_=w1_bf[:].rearrange("p t m j -> p (t m j)")
+        )
+
+        picked_words = [tile([P, V], U16, f"picked_words{d}") for d in range(PIECES)]
+        for d in range(PIECES):
+            nc.vector.tensor_copy(
+                picked_words[d][:], word_table[:].indirect(offsets[:, d * (V // 16) : (d + 1) * (V // 16)])
+            )
+
+        def part(c):
+            return slice(c * WIDE, (c + 1) * WIDE)
+
+        h = [tile([P, CHUNKS * WIDE], F32, f"h{d}") for d in range(PIECES)]
+        for d, c in ((0, 0), (1, 0), (0, 1), (1, 1), (2, 0), (2, 1)):
+            pre = ps.tile([P, PACK, SEG], F32, name=f"pre{d}{c}")
+            first = d * V + c * SEG
+            for t in range(PACK):
+                nc.tensor.matmul_mx(
+                    out=pre[:, t, :],
+                    lhsT=w1_codes[:, t * P : (t + 1) * P].bitcast(FP8X4),
+                    lhsT_scale=w1_scales[:, t * P : (t + 1) * P],
+                    rhs=picked_words[d][:, c * SEG : (c + 1) * SEG].bitcast(FP4X4),
+                    rhs_scale=picked_scales[:, first : first + SEG],
+                    start=True,
+                    stop=True,
+                )
+            nc.scalar.activation(
+                h[d][:, part(c)].rearrange("p (v t) -> p v t", t=PACK),
+                pre[:].rearrange("p t v -> p v t"),
+                ACT.Gelu_apprx_tanh,
+            )
+
+        w23_bf = tile([P, 2, N, PACK], BF16, "w23_bf")
+        w23_codes = tile([P, 2 * N], U32, "w23_codes")
+        w23_scales = tile([P, 2 * N], U8, "w23_scales")
+
+        def round_w23(u, engine):
+            if engine == "scalar":
+                nc.scalar.activation(w23_bf[:, u, :, :], w23_raw[u][:].rearrange("p j n -> p n j"), ACT.Identity, bias=zero[:])
+            elif engine == "gpsimd":
+                nc.gpsimd.tensor_copy(w23_bf[:, u, :, :], w23_raw[u][:].rearrange("p j n -> p n j"))
+            else:
+                nc.vector.tensor_copy(
+                    w23_bf[:, u, :, :].rearrange("p (c i) j -> p c j i", i=4),
+                    w23_raw[u][:].rearrange("p j (c i) -> p c j i", i=4),
+                )
+
+        def quantise_w23():
+            nc.vector.quantize_mx(
+                out=w23_codes[:].bitcast(FP8X4), scales=w23_scales[:], in_=w23_bf[:].rearrange("p u n j -> p (u n j)")
+            )
+
+        pair_sum = tile([P, CHUNKS * WIDE], F32, "pair_sum")
+        pair_diff = tile([P, CHUNKS * WIDE], F32, "pair_diff")
+        bend = tile([P, CHUNKS * WIDE], F32, "bend")
+        diff_sq = tile([P, CHUNKS * WIDE], F32, "diff_sq")
+        bend_sq = tile([P, CHUNKS * WIDE], F32, "bend_sq")
+        spread = tile([P, CHUNKS * WIDE], F32, "spread")
+        stat_bf = [tile([P, CHUNKS * WIDE], BF16, f"stat_bf{u}") for u in range(2)]
+        stat_codes = [tile([P, V], U32, f"stat_codes{u}") for u in range(2)]
+        stat_scales = [tile([P, V], U8, f"stat_scales{u}") for u in range(2)]
+        both = slice(0, CHUNKS * WIDE)
+
+        def make_sum(s):
+            nc.vector.tensor_tensor(pair_sum[:, s], h[0][:, s], h[1][:, s], ALU.add)
+
+        def make_diff(s):
+            nc.vector.tensor_tensor(pair_diff[:, s], h[0][:, s], h[1][:, s], ALU.subtract)
+
+        def make_bend(s):
+            nc.vector.scalar_tensor_tensor(bend[:, s], h[2][:, s], -2.0, pair_sum[:, s], ALU.mult, ALU.add)
+
+        def make_mean(s):
+            nc.vector.scalar_tensor_tensor(stat_bf[0][:, s], bend[:, s], 1.0 / 3.0, h[2][:, s], ALU.mult, ALU.add)
+
+        def square_diff(s):
+            nc.scalar.activation(diff_sq[:, s], pair_diff[:, s], ACT.Square, scale=math.sqrt(3.0))
+
+        def square_bend_scalar(s):
+            nc.scalar.activation(bend_sq[:, s], bend[:, s], ACT.Square)
+
+        def square_bend_vector(s):
+            nc.vector.tensor_tensor(bend_sq[:, s], bend[:, s], bend[:, s], ALU.mult)
+
+        def make_spread(s):
+            nc.vector.scalar_tensor_tensor(spread[:, s], diff_sq[:, s], SQRT_FLOOR, bend_sq[:, s], ALU.max, ALU.add)
+
+        def make_dev(s):
+            nc.scalar.activation(stat_bf[1][:, s], spread[:, s], ACT.Sqrt, scale=1.0 / 18.0)
+
+        def quantise(u, s):
+            cols = slice(s.start // PACK, s.stop // PACK)
+            nc.vector.quantize_mx(
+                out=stat_codes[u][:, cols].bitcast(FP8X4), scales=stat_scales[u][:, cols], in_=stat_bf[u][:, s]
+            )
+
+        def finish(c, engine):
+            acc = ps.tile([P, SEG], F32, name=f"acc{c}")
+            cols = slice(c * SEG, (c + 1) * SEG)
+            for u in range(2):
+                nc.tensor.matmul_mx(
+                    out=acc[:],
+                    lhsT=w23_codes[:, u * N : (u + 1) * N].bitcast(FP8X4),
+                    lhsT_scale=w23_scales[:, u * N : (u + 1) * N],
+                    rhs=stat_codes[u][:, cols].bitcast(FP8X4),
+                    rhs_scale=stat_scales[u][:, cols],
+                    start=(u == 0),
+                    stop=(u == 1),
+                )
+            result = tile([P, SEG], F32, f"result{c}")
+            if engine == "scalar":
+                nc.scalar.copy(result[:], acc[:])
+            else:
+                nc.vector.tensor_copy(result[:], acc[:])
+            nc.sync.dma_start(out[:, cols], result[:])
+
+        round_w23(0, "vector")
+        round_w23(1, "vector")
+        make_sum(part(0))
+        quantise_w23()
+        make_diff(part(0))
+        make_sum(part(1))
+        make_diff(part(1))
+        make_bend(part(0))
+        make_bend(part(1))
+        square_diff(both)
+        square_bend_scalar(part(0))
+        square_bend_vector(part(1))
+        make_spread(part(0))
+        make_spread(part(1))
+        make_mean(both)
+        make_dev(part(0))
+        make_dev(part(1))
+        quantise(0, both)
+        quantise(1, part(0))
+        finish(0, "vector")
+        quantise(1, part(1))
+        finish(1, "scalar")

@@ -107,11 +107,13 @@ def tile_picked_statpool_gelu_p_kernel(tc, x_words, x_scales, w1, w2, w3, offs, 
                     start=True,
                     stop=True,
                 )
-            nc.scalar.activation(
-                h[d][:, part(c)].rearrange("p (v t) -> p v t", t=PACK),
-                pre[:].rearrange("p t v -> p v t"),
-                ACT.Gelu_apprx_tanh,
-            )
+            step = SEG // 2 if d == 1 else SEG
+            for v0 in range(0, SEG, step):
+                nc.scalar.activation(
+                    h[d][:, part(c)].rearrange("p (v t) -> p v t", t=PACK)[:, v0 : v0 + step, :],
+                    pre[:].rearrange("p t v -> p v t")[:, v0 : v0 + step, :],
+                    ACT.Gelu_apprx_tanh,
+                )
 
         w23_bf = tile([P, 2, N, PACK], BF16, "w23_bf")
         w23_codes = tile([P, 2 * N], U32, "w23_codes")
@@ -119,7 +121,10 @@ def tile_picked_statpool_gelu_p_kernel(tc, x_words, x_scales, w1, w2, w3, offs, 
 
         def round_w23(u, engine):
             if engine == "scalar":
-                nc.scalar.activation(w23_bf[:, u, :, :], w23_raw[u][:].rearrange("p j n -> p n j"), ACT.Identity, bias=zero[:])
+                nc.scalar.copy(
+                    w23_bf[:, u, :, :].rearrange("p (c i) j -> p c j i", i=4),
+                    w23_raw[u][:].rearrange("p j (c i) -> p c j i", i=4),
+                )
             elif engine == "gpsimd":
                 nc.gpsimd.tensor_copy(w23_bf[:, u, :, :], w23_raw[u][:].rearrange("p j n -> p n j"))
             else:
@@ -197,25 +202,25 @@ def tile_picked_statpool_gelu_p_kernel(tc, x_words, x_scales, w1, w2, w3, offs, 
                 nc.vector.tensor_copy(result[:], acc[:])
             nc.sync.dma_start(out[:, cols], result[:])
 
-        round_w23(0, "vector")
+        round_w23(0, "scalar")
         round_w23(1, "vector")
-        make_sum(part(0))
         quantise_w23()
-        make_diff(part(0))
-        make_sum(part(1))
-        make_diff(part(1))
+        for q0 in range(0, 2 * WIDE, WIDE // 2): make_sum(slice(q0, q0 + WIDE // 2)); make_diff(slice(q0, q0 + WIDE // 2))
         make_bend(part(0))
         make_bend(part(1))
-        square_diff(both)
+        square_diff(part(0))
+        square_diff(part(1))
         square_bend_scalar(part(0))
+        make_mean(part(0))
         square_bend_vector(part(1))
         make_spread(part(0))
         make_spread(part(1))
-        make_mean(both)
+        quantise(0, part(0))
+        make_mean(part(1))
         make_dev(part(0))
         make_dev(part(1))
-        quantise(0, both)
         quantise(1, part(0))
-        finish(0, "vector")
+        quantise(0, part(1))
         quantise(1, part(1))
+        finish(0, "scalar")
         finish(1, "scalar")

@@ -2,6 +2,7 @@ import math
 from contextlib import ExitStack
 
 import concourse.mybir as mybir
+from concourse.masks import make_identity
 
 K, T, S, V, H, N = 512, 2048, 768, 256, 512, 128
 FLOPS = 2 * K * H * S + 2 * 2 * H * N * V
@@ -22,9 +23,10 @@ PACK = 4
 PIECES = 3
 SEG = 128
 CHUNKS = V // SEG
-WIDE = SEG * PACK
-W1_CUTS = ((0, 128), (128, 256), (256, 384), (384, 512))
-W1_AHEAD = 2
+QUARTER = H // 4
+HALF = H // 2
+RUN = HALF // PACK
+W1_AHEAD = 1
 SQRT_FLOOR = 2.0 ** -110
 
 
@@ -32,10 +34,14 @@ def tile_picked_statpool_gelu_p_kernel(tc, x_words, x_scales, w1, w2, w3, offs, 
     nc = tc.nc
     with ExitStack() as ctx:
         sb = ctx.enter_context(tc.tile_pool(name="sb", bufs=1))
+        reuse = ctx.enter_context(tc.tile_pool(name="reuse", bufs=1))
         ps = ctx.enter_context(tc.psum_pool(name="ps", bufs=1))
 
-        def tile(shape, dtype, name, tag=""):
-            return sb.tile(shape, dtype, name=name, tag=tag, align_bytes=64)
+        def tile(shape, dtype, name):
+            return sb.tile(shape, dtype, name=name, align_bytes=64)
+
+        def bank(shape, name, number):
+            return ps.tile(shape, F32, name=name, tag=f"bank{number}")
 
         offsets = sb.tile([P, S // 16], U16, name="offsets")
         nc.sync.dma_start(offsets[:], offs)
@@ -47,180 +53,209 @@ def tile_picked_statpool_gelu_p_kernel(tc, x_words, x_scales, w1, w2, w3, offs, 
         zero = tile([P, 1], F32, "zero")
         nc.gpsimd.memset(zero_in[:], 0.0)
         nc.scalar.activation(zero[:], zero_in[:], ACT.Gelu_apprx_tanh)
+        floor = tile([P, 1], F32, "floor")
+        nc.gpsimd.memset(floor[:], SQRT_FLOOR)
+        identity = tile([P, P], F32, "identity")
+        make_identity(nc, identity[:])
 
-        w1_rows = w1.rearrange("(p j) c -> p j c", j=PACK)
-        w1_raw = [tile([P, PACK, hi - lo], F32, f"w1_raw{u}") for u, (lo, hi) in enumerate(W1_CUTS)]
-
-        def load_w1(u):
-            lo, hi = W1_CUTS[u]
-            nc.sync.dma_start(w1_raw[u][:], w1_rows[:, :, lo:hi])
-
-        for u in range(W1_AHEAD):
-            load_w1(u)
-        for r in range(4):
-            nc.sync.dma_start(scale_table[r:P:32, :].bitcast(I32), x_scales[0, r:16:4, :].bitcast(I32))
-        for u in range(W1_AHEAD, len(W1_CUTS)):
-            load_w1(u)
         word_table = tile([P, T], U16, "word_table")
         nc.sync.dma_start(word_table[:].bitcast(I32), x_words[0].bitcast(I32))
+
+        raw_bytes = 4 * PACK * QUARTER
+        w1_rows = w1.rearrange("(p j) c -> p j c", j=PACK)
+        w1_raw = [
+            reuse.tile([P, PACK, QUARTER], F32, name=f"w1_raw{q}", align_bytes=64, offset=raw_bytes * q) for q in range(4)
+        ]
+
+        def load_w1(q):
+            nc.sync.dma_start(w1_raw[q][:], w1_rows[:, :, q * QUARTER : (q + 1) * QUARTER])
+
+        for q in range(W1_AHEAD):
+            load_w1(q)
+        for r in range(4):
+            nc.sync.dma_start(scale_table[r:P:32, :].bitcast(I32), x_scales[0, r:16:4, :].bitcast(I32))
+        for q in range(W1_AHEAD, 4):
+            load_w1(q)
         w23_raw = [tile([P, PACK, N], F32, f"w23_raw{u}") for u in range(2)]
         for u, w in enumerate((w2, w3)):
             nc.sync.dma_start(w23_raw[u][:], w.rearrange("(p j) n -> p j n", j=PACK))
 
-        picked_scales = tile([P, S], U8, "picked_scales")
-        nc.vector.tensor_copy(picked_scales[:], scale_table[:].indirect(offsets[:]))
+        picked_words = [tile([P, V], U16, f"picked_words{d}") for d in range(2)]
+        picked_words.append(reuse.tile([P, V], U16, name="picked_words2", align_bytes=64, offset=raw_bytes))
+        early_scales = tile([P, 2 * V], U8, "early_scales")
+        late_scales = reuse.tile([P, V], U8, name="late_scales", align_bytes=64, offset=3 * raw_bytes)
+        picked_scales = [early_scales[:, :V], early_scales[:, V:], late_scales[:]]
 
-        w1_bf = tile([P, PACK, P, PACK], BF16, "w1_bf")
-        for u, (lo, hi) in enumerate(W1_CUTS):
-            nc.scalar.activation(
-                w1_bf[:, :, lo // PACK : hi // PACK, :].rearrange("p t m j -> p m j t"),
-                w1_raw[u][:].rearrange("p j (m t) -> p m j t", t=PACK),
-                ACT.Identity,
-                bias=zero[:],
-            )
-        w1_codes = tile([P, H], U32, "w1_codes")
-        w1_scales = tile([P, H], U8, "w1_scales")
-        nc.vector.quantize_mx(
-            out=w1_codes[:].bitcast(FP8X4), scales=w1_scales[:], in_=w1_bf[:].rearrange("p t m j -> p (t m j)")
-        )
-
-        picked_words = [tile([P, V], U16, f"picked_words{d}") for d in range(PIECES)]
-        for d in range(PIECES):
+        def gather_words(d):
             nc.vector.tensor_copy(
                 picked_words[d][:], word_table[:].indirect(offsets[:, d * (V // 16) : (d + 1) * (V // 16)])
             )
 
-        def part(c):
-            return slice(c * WIDE, (c + 1) * WIDE)
+        w1_bf = [tile([P, PACK, RUN, PACK], BF16, f"w1_bf{u}") for u in range(2)]
+        w1_codes = tile([P, H], U32, "w1_codes")
+        w1_scales = tile([P, H], U8, "w1_scales")
 
-        h = [tile([P, CHUNKS * WIDE], F32, f"h{d}") for d in range(PIECES)]
-        for d, c in ((0, 0), (1, 0), (0, 1), (1, 1), (2, 0), (2, 1)):
-            pre = ps.tile([P, PACK, SEG], F32, name=f"pre{d}{c}")
-            first = d * V + c * SEG
-            for t in range(PACK):
-                nc.tensor.matmul_mx(
-                    out=pre[:, t, :],
-                    lhsT=w1_codes[:, t * P : (t + 1) * P].bitcast(FP8X4),
-                    lhsT_scale=w1_scales[:, t * P : (t + 1) * P],
-                    rhs=picked_words[d][:, c * SEG : (c + 1) * SEG].bitcast(FP4X4),
-                    rhs_scale=picked_scales[:, first : first + SEG],
-                    start=True,
-                    stop=True,
-                )
-            step = SEG // 2 if d == 1 else SEG
-            for v0 in range(0, SEG, step):
-                nc.scalar.activation(
-                    h[d][:, part(c)].rearrange("p (v t) -> p v t", t=PACK)[:, v0 : v0 + step, :],
-                    pre[:].rearrange("p t v -> p v t")[:, v0 : v0 + step, :],
-                    ACT.Gelu_apprx_tanh,
-                )
+        def round_w1(q):
+            m0 = (q % 2) * (QUARTER // PACK)
+            nc.scalar.activation(
+                w1_bf[q // 2][:, :, m0 : m0 + QUARTER // PACK, :].rearrange("p t m j -> p m j t"),
+                w1_raw[q][:].rearrange("p j (m t) -> p m j t", t=PACK),
+                ACT.Identity,
+                bias=zero[:],
+            )
+
+        def quantise_w1(u):
+            cols = slice(u * HALF, (u + 1) * HALF)
+            nc.vector.quantize_mx(
+                out=w1_codes[:, cols].bitcast(FP8X4),
+                scales=w1_scales[:, cols],
+                in_=w1_bf[u][:].rearrange("p t m j -> p (t m j)"),
+            )
+
+        gather_words(0)
+        gather_words(1)
+        nc.vector.tensor_copy(early_scales[:], scale_table[:].indirect(offsets[:, : 2 * V // 16]))
+        round_w1(0)
+        round_w1(1)
+        quantise_w1(0)
+        gather_words(2)
+        round_w1(2)
+        round_w1(3)
+        quantise_w1(1)
+        nc.vector.tensor_copy(late_scales[:], scale_table[:].indirect(offsets[:, 2 * V // 16 :]))
+
+        h01 = [tile([P, 2, PACK, 2, RUN], F32, f"h01_{c}") for c in range(CHUNKS)]
+        h2 = [tile([P, PACK, 2, RUN], F32, f"h2_{c}") for c in range(CHUNKS)]
+
+        def product(dst, d, c, cols):
+            nc.tensor.matmul_mx(
+                out=dst,
+                lhsT=picked_words[d][:, c * SEG : (c + 1) * SEG].bitcast(FP4X4),
+                lhsT_scale=picked_scales[d][:, c * SEG : (c + 1) * SEG],
+                rhs=w1_codes[:, cols].bitcast(FP8X4),
+                rhs_scale=w1_scales[:, cols],
+                start=True,
+                stop=True,
+            )
+
+        for d in range(2):
+            pre = bank([P, PACK, RUN], f"pre_first{d}", d)
+            product(pre[:].rearrange("p t m -> p (t m)"), d, 0, slice(0, HALF))
+            nc.scalar.activation(h01[0][:, d, :, 0, :], pre[:], ACT.Gelu_apprx_tanh)
+        for number, (c, u) in enumerate(((1, 0), (0, 1), (1, 1))):
+            pre = bank([P, 2, PACK, RUN], f"pre{c}{u}", 2 + number)
+            for d in range(2):
+                product(pre[:, d].rearrange("p t m -> p (t m)"), d, c, slice(u * HALF, (u + 1) * HALF))
+            nc.scalar.activation(h01[c][:, :, :, u, :], pre[:], ACT.Gelu_apprx_tanh)
+        for c in range(CHUNKS):
+            pre = bank([P, 2, PACK, RUN], f"pre_last{c}", 5 + c)
+            product(pre[:].rearrange("p u t m -> p (u t m)"), 2, c, slice(0, H))
+            nc.scalar.activation(h2[c][:].rearrange("p t u m -> p u t m"), pre[:], ACT.Gelu_apprx_tanh)
 
         w23_bf = tile([P, 2, N, PACK], BF16, "w23_bf")
         w23_codes = tile([P, 2 * N], U32, "w23_codes")
         w23_scales = tile([P, 2 * N], U8, "w23_scales")
+        for u in range(2):
+            nc.vector.tensor_copy(
+                w23_bf[:, u, :, :].rearrange("p (c i) j -> p c j i", i=4),
+                w23_raw[u][:].rearrange("p j (c i) -> p c j i", i=4),
+            )
+        nc.vector.quantize_mx(
+            out=w23_codes[:].bitcast(FP8X4), scales=w23_scales[:], in_=w23_bf[:].rearrange("p u n j -> p (u n j)")
+        )
 
-        def round_w23(u, engine):
-            if engine == "scalar":
-                nc.scalar.copy(
-                    w23_bf[:, u, :, :].rearrange("p (c i) j -> p c j i", i=4),
-                    w23_raw[u][:].rearrange("p j (c i) -> p c j i", i=4),
-                )
-            elif engine == "gpsimd":
-                nc.gpsimd.tensor_copy(w23_bf[:, u, :, :], w23_raw[u][:].rearrange("p j n -> p n j"))
-            else:
-                nc.vector.tensor_copy(
-                    w23_bf[:, u, :, :].rearrange("p (c i) j -> p c j i", i=4),
-                    w23_raw[u][:].rearrange("p j (c i) -> p c j i", i=4),
+        def stat(name):
+            return [tile([P, PACK, 2, RUN], F32, f"{name}{c}") for c in range(CHUNKS)]
+
+        pair_sum, pair_diff, bend, diff_sq, bend_sq = (
+            stat(name) for name in ("pair_sum", "pair_diff", "bend", "diff_sq", "bend_sq")
+        )
+        stat_bf = [[tile([P, SEG, PACK], BF16, f"stat_bf{k}{c}") for c in range(CHUNKS)] for k in range(2)]
+        stat_codes = [tile([P, V], U32, f"stat_codes{k}") for k in range(2)]
+        stat_scales = [tile([P, V], U8, f"stat_scales{k}") for k in range(2)]
+
+        def flat(t):
+            return t[:].rearrange("p t u m -> p (t u m)")
+
+        def make_pair(c, u):
+            nc.vector.tensor_tensor(pair_sum[c][:, :, u, :], h01[c][:, 0, :, u, :], h01[c][:, 1, :, u, :], ALU.add)
+            nc.vector.tensor_tensor(pair_diff[c][:, :, u, :], h01[c][:, 0, :, u, :], h01[c][:, 1, :, u, :], ALU.subtract)
+
+        def make_bend(c):
+            nc.vector.scalar_tensor_tensor(flat(bend[c]), flat(h2[c]), -2.0, flat(pair_sum[c]), ALU.mult, ALU.add)
+
+        def square_diff(c):
+            nc.scalar.activation(flat(diff_sq[c]), flat(pair_diff[c]), ACT.Square, scale=math.sqrt(3.0))
+
+        def square_bend(c):
+            nc.vector.tensor_tensor(flat(bend_sq[c]), flat(bend[c]), flat(bend[c]), ALU.mult)
+
+        def turn(dst, src, first):
+            for t in range(PACK):
+                nc.tensor.matmul(
+                    dst[:, t, :],
+                    flat(src)[:, t * P : (t + 1) * P],
+                    identity[:],
+                    start=first and t == 0,
+                    stop=not first and t == PACK - 1,
+                    is_transpose=True,
                 )
 
-        def quantise_w23():
-            nc.vector.quantize_mx(
-                out=w23_codes[:].bitcast(FP8X4), scales=w23_scales[:], in_=w23_bf[:].rearrange("p u n j -> p (u n j)")
+        total = [bank([P, PACK, SEG], f"total{c}", (7, 0)[c]) for c in range(CHUNKS)]
+        spread = [bank([P, PACK, SEG], f"spread{c}", 1 + c) for c in range(CHUNKS)]
+
+        def make_mean(c):
+            nc.vector.tensor_scalar_mul(stat_bf[0][c][:], total[c][:].rearrange("p t v -> p v t"), 1.0 / 3.0)
+
+        def make_dev(c):
+            nc.scalar.activation(
+                stat_bf[1][c][:], spread[c][:].rearrange("p t v -> p v t"), ACT.Sqrt, scale=1.0 / 18.0, bias=floor[:]
             )
 
-        pair_sum = tile([P, CHUNKS * WIDE], F32, "pair_sum")
-        pair_diff = tile([P, CHUNKS * WIDE], F32, "pair_diff")
-        bend = tile([P, CHUNKS * WIDE], F32, "bend")
-        diff_sq = tile([P, CHUNKS * WIDE], F32, "diff_sq")
-        bend_sq = tile([P, CHUNKS * WIDE], F32, "bend_sq")
-        spread = tile([P, CHUNKS * WIDE], F32, "spread")
-        stat_bf = [tile([P, CHUNKS * WIDE], BF16, f"stat_bf{u}") for u in range(2)]
-        stat_codes = [tile([P, V], U32, f"stat_codes{u}") for u in range(2)]
-        stat_scales = [tile([P, V], U8, f"stat_scales{u}") for u in range(2)]
-        both = slice(0, CHUNKS * WIDE)
-
-        def make_sum(s):
-            nc.vector.tensor_tensor(pair_sum[:, s], h[0][:, s], h[1][:, s], ALU.add)
-
-        def make_diff(s):
-            nc.vector.tensor_tensor(pair_diff[:, s], h[0][:, s], h[1][:, s], ALU.subtract)
-
-        def make_bend(s):
-            nc.vector.scalar_tensor_tensor(bend[:, s], h[2][:, s], -2.0, pair_sum[:, s], ALU.mult, ALU.add)
-
-        def make_mean(s):
-            nc.vector.scalar_tensor_tensor(stat_bf[0][:, s], bend[:, s], 1.0 / 3.0, h[2][:, s], ALU.mult, ALU.add)
-
-        def square_diff(s):
-            nc.scalar.activation(diff_sq[:, s], pair_diff[:, s], ACT.Square, scale=math.sqrt(3.0))
-
-        def square_bend_scalar(s):
-            nc.scalar.activation(bend_sq[:, s], bend[:, s], ACT.Square)
-
-        def square_bend_vector(s):
-            nc.vector.tensor_tensor(bend_sq[:, s], bend[:, s], bend[:, s], ALU.mult)
-
-        def make_spread(s):
-            nc.vector.scalar_tensor_tensor(spread[:, s], diff_sq[:, s], SQRT_FLOOR, bend_sq[:, s], ALU.max, ALU.add)
-
-        def make_dev(s):
-            nc.scalar.activation(stat_bf[1][:, s], spread[:, s], ACT.Sqrt, scale=1.0 / 18.0)
-
-        def quantise(u, s):
-            cols = slice(s.start // PACK, s.stop // PACK)
-            nc.vector.quantize_mx(
-                out=stat_codes[u][:, cols].bitcast(FP8X4), scales=stat_scales[u][:, cols], in_=stat_bf[u][:, s]
-            )
-
-        def finish(c, engine):
-            acc = ps.tile([P, SEG], F32, name=f"acc{c}")
+        def quantise(k, c):
             cols = slice(c * SEG, (c + 1) * SEG)
-            for u in range(2):
+            nc.vector.quantize_mx(
+                out=stat_codes[k][:, cols].bitcast(FP8X4),
+                scales=stat_scales[k][:, cols],
+                in_=stat_bf[k][c][:].rearrange("p v t -> p (v t)"),
+            )
+
+        def finish(c):
+            acc = bank([P, SEG], f"acc{c}", 3 + c)
+            cols = slice(c * SEG, (c + 1) * SEG)
+            for k in range(2):
                 nc.tensor.matmul_mx(
                     out=acc[:],
-                    lhsT=w23_codes[:, u * N : (u + 1) * N].bitcast(FP8X4),
-                    lhsT_scale=w23_scales[:, u * N : (u + 1) * N],
-                    rhs=stat_codes[u][:, cols].bitcast(FP8X4),
-                    rhs_scale=stat_scales[u][:, cols],
-                    start=(u == 0),
-                    stop=(u == 1),
+                    lhsT=w23_codes[:, k * N : (k + 1) * N].bitcast(FP8X4),
+                    lhsT_scale=w23_scales[:, k * N : (k + 1) * N],
+                    rhs=stat_codes[k][:, cols].bitcast(FP8X4),
+                    rhs_scale=stat_scales[k][:, cols],
+                    start=(k == 0),
+                    stop=(k == 1),
                 )
             result = tile([P, SEG], F32, f"result{c}")
-            if engine == "scalar":
-                nc.scalar.copy(result[:], acc[:])
-            else:
-                nc.vector.tensor_copy(result[:], acc[:])
+            nc.scalar.copy(result[:], acc[:])
             nc.sync.dma_start(out[:, cols], result[:])
 
-        round_w23(0, "scalar")
-        round_w23(1, "vector")
-        quantise_w23()
-        for q0 in range(0, 2 * WIDE, WIDE // 2): make_sum(slice(q0, q0 + WIDE // 2)); make_diff(slice(q0, q0 + WIDE // 2))
-        make_bend(part(0))
-        make_bend(part(1))
-        square_diff(part(0))
-        square_diff(part(1))
-        square_bend_scalar(part(0))
-        make_mean(part(0))
-        square_bend_vector(part(1))
-        make_spread(part(0))
-        make_spread(part(1))
-        quantise(0, part(0))
-        make_mean(part(1))
-        make_dev(part(0))
-        make_dev(part(1))
-        quantise(1, part(0))
-        quantise(0, part(1))
-        quantise(1, part(1))
-        finish(0, "scalar")
-        finish(1, "scalar")
+        for c, u in ((0, 0), (1, 0), (0, 1), (1, 1)):
+            make_pair(c, u)
+        for c in range(CHUNKS):
+            make_bend(c)
+        for c in range(CHUNKS):
+            square_diff(c)
+            turn(total[c], pair_sum[c], True)
+            turn(total[c], h2[c], False)
+        for c in range(CHUNKS):
+            square_bend(c)
+        for c in range(CHUNKS):
+            turn(spread[c], diff_sq[c], True)
+            turn(spread[c], bend_sq[c], False)
+        for c in range(CHUNKS):
+            make_mean(c)
+        for c in range(CHUNKS):
+            make_dev(c)
+            quantise(0, c)
+        for c in range(CHUNKS):
+            quantise(1, c)
+        for c in range(CHUNKS):
+            finish(c)

@@ -43,6 +43,8 @@ def tile_picked_statpool_gelu_p_kernel(tc, x_words, x_scales, w1, w2, w3, offs, 
         def bank(shape, name, number):
             return ps.tile(shape, F32, name=name, tag=f"bank{number}")
 
+        word_table = tile([P, T], U16, "word_table")
+        nc.sync.dma_start(word_table[:].bitcast(I32), x_words[0].bitcast(I32))
         offsets = sb.tile([P, S // 16], U16, name="offsets")
         nc.sync.dma_start(offsets[:], offs)
 
@@ -57,9 +59,6 @@ def tile_picked_statpool_gelu_p_kernel(tc, x_words, x_scales, w1, w2, w3, offs, 
         nc.gpsimd.memset(floor[:], SQRT_FLOOR)
         identity = tile([P, P], F32, "identity")
         make_identity(nc, identity[:])
-
-        word_table = tile([P, T], U16, "word_table")
-        nc.sync.dma_start(word_table[:].bitcast(I32), x_words[0].bitcast(I32))
 
         raw_bytes = 4 * PACK * QUARTER
         w1_rows = w1.rearrange("(p j) c -> p j c", j=PACK)
@@ -80,16 +79,12 @@ def tile_picked_statpool_gelu_p_kernel(tc, x_words, x_scales, w1, w2, w3, offs, 
         for u, w in enumerate((w2, w3)):
             nc.sync.dma_start(w23_raw[u][:], w.rearrange("(p j) n -> p j n", j=PACK))
 
-        picked_words = [tile([P, V], U16, f"picked_words{d}") for d in range(2)]
-        picked_words.append(reuse.tile([P, V], U16, name="picked_words2", align_bytes=64, offset=raw_bytes))
+        early_words = tile([P, 2 * V], U16, "early_words")
+        late_words = reuse.tile([P, V], U16, name="late_words", align_bytes=64, offset=raw_bytes)
+        picked_words = [early_words[:, :V], early_words[:, V:], late_words[:]]
         early_scales = tile([P, 2 * V], U8, "early_scales")
         late_scales = reuse.tile([P, V], U8, name="late_scales", align_bytes=64, offset=3 * raw_bytes)
         picked_scales = [early_scales[:, :V], early_scales[:, V:], late_scales[:]]
-
-        def gather_words(d):
-            nc.vector.tensor_copy(
-                picked_words[d][:], word_table[:].indirect(offsets[:, d * (V // 16) : (d + 1) * (V // 16)])
-            )
 
         w1_bf = [tile([P, PACK, RUN, PACK], BF16, f"w1_bf{u}") for u in range(2)]
         w1_codes = tile([P, H], U32, "w1_codes")
@@ -112,13 +107,12 @@ def tile_picked_statpool_gelu_p_kernel(tc, x_words, x_scales, w1, w2, w3, offs, 
                 in_=w1_bf[u][:].rearrange("p t m j -> p (t m j)"),
             )
 
-        gather_words(0)
-        gather_words(1)
+        nc.vector.tensor_copy(early_words[:], word_table[:].indirect(offsets[:, : 2 * V // 16]))
         nc.vector.tensor_copy(early_scales[:], scale_table[:].indirect(offsets[:, : 2 * V // 16]))
         round_w1(0)
         round_w1(1)
         quantise_w1(0)
-        gather_words(2)
+        nc.vector.tensor_copy(late_words[:], word_table[:].indirect(offsets[:, 2 * V // 16 :]))
         round_w1(2)
         round_w1(3)
         quantise_w1(1)
@@ -138,12 +132,8 @@ def tile_picked_statpool_gelu_p_kernel(tc, x_words, x_scales, w1, w2, w3, offs, 
                 stop=True,
             )
 
-        for d in range(2):
-            pre = bank([P, PACK, RUN], f"pre_first{d}", d)
-            product(pre[:].rearrange("p t m -> p (t m)"), d, 0, slice(0, HALF))
-            nc.scalar.activation(h01[0][:, d, :, 0, :], pre[:], ACT.Gelu_apprx_tanh)
-        for number, (c, u) in enumerate(((1, 0), (0, 1), (1, 1))):
-            pre = bank([P, 2, PACK, RUN], f"pre{c}{u}", 2 + number)
+        for number, (c, u) in enumerate(((0, 0), (1, 0), (0, 1), (1, 1))):
+            pre = bank([P, 2, PACK, RUN], f"pre{c}{u}", 1 + number)
             for d in range(2):
                 product(pre[:, d].rearrange("p t m -> p (t m)"), d, c, slice(u * HALF, (u + 1) * HALF))
             nc.scalar.activation(h01[c][:, :, :, u, :], pre[:], ACT.Gelu_apprx_tanh)
@@ -160,9 +150,6 @@ def tile_picked_statpool_gelu_p_kernel(tc, x_words, x_scales, w1, w2, w3, offs, 
                 w23_bf[:, u, :, :].rearrange("p (c i) j -> p c j i", i=4),
                 w23_raw[u][:].rearrange("p j (c i) -> p c j i", i=4),
             )
-        nc.vector.quantize_mx(
-            out=w23_codes[:].bitcast(FP8X4), scales=w23_scales[:], in_=w23_bf[:].rearrange("p u n j -> p (u n j)")
-        )
 
         def stat(name):
             return [tile([P, PACK, 2, RUN], F32, f"{name}{c}") for c in range(CHUNKS)]
@@ -250,6 +237,9 @@ def tile_picked_statpool_gelu_p_kernel(tc, x_words, x_scales, w1, w2, w3, offs, 
         for c in range(CHUNKS):
             turn(spread[c], diff_sq[c], True)
             turn(spread[c], bend_sq[c], False)
+        nc.vector.quantize_mx(
+            out=w23_codes[:].bitcast(FP8X4), scales=w23_scales[:], in_=w23_bf[:].rearrange("p u n j -> p (u n j)")
+        )
         for c in range(CHUNKS):
             make_mean(c)
         for c in range(CHUNKS):

@@ -79,12 +79,16 @@ def tile_picked_statpool_gelu_p_kernel(tc, x_words, x_scales, w1, w2, w3, offs, 
         for u, w in enumerate((w2, w3)):
             nc.sync.dma_start(w23_raw[u][:], w.rearrange("(p j) n -> p j n", j=PACK))
 
-        early_words = tile([P, 2 * V], U16, "early_words")
-        late_words = reuse.tile([P, V], U16, name="late_words", align_bytes=64, offset=raw_bytes)
-        picked_words = [early_words[:, :V], early_words[:, V:], late_words[:]]
+        picked_words = [tile([P, V], U16, f"picked_words{d}") for d in range(2)]
+        picked_words.append(reuse.tile([P, V], U16, name="picked_words2", align_bytes=64, offset=raw_bytes))
         early_scales = tile([P, 2 * V], U8, "early_scales")
         late_scales = reuse.tile([P, V], U8, name="late_scales", align_bytes=64, offset=3 * raw_bytes)
         picked_scales = [early_scales[:, :V], early_scales[:, V:], late_scales[:]]
+
+        def gather_words(d):
+            nc.vector.tensor_copy(
+                picked_words[d][:], word_table[:].indirect(offsets[:, d * (V // 16) : (d + 1) * (V // 16)])
+            )
 
         w1_bf = [tile([P, PACK, RUN, PACK], BF16, f"w1_bf{u}") for u in range(2)]
         w1_codes = tile([P, H], U32, "w1_codes")
@@ -107,12 +111,13 @@ def tile_picked_statpool_gelu_p_kernel(tc, x_words, x_scales, w1, w2, w3, offs, 
                 in_=w1_bf[u][:].rearrange("p t m j -> p (t m j)"),
             )
 
-        nc.vector.tensor_copy(early_words[:], word_table[:].indirect(offsets[:, : 2 * V // 16]))
+        gather_words(0)
+        gather_words(1)
         nc.vector.tensor_copy(early_scales[:], scale_table[:].indirect(offsets[:, : 2 * V // 16]))
         round_w1(0)
         round_w1(1)
         quantise_w1(0)
-        nc.vector.tensor_copy(late_words[:], word_table[:].indirect(offsets[:, 2 * V // 16 :]))
+        gather_words(2)
         round_w1(2)
         round_w1(3)
         quantise_w1(1)
@@ -132,11 +137,19 @@ def tile_picked_statpool_gelu_p_kernel(tc, x_words, x_scales, w1, w2, w3, offs, 
                 stop=True,
             )
 
-        for number, (c, u) in enumerate(((0, 0), (1, 0), (0, 1), (1, 1))):
-            pre = bank([P, 2, PACK, RUN], f"pre{c}{u}", 1 + number)
+        def pair(c, u, number):
+            pre = bank([P, 2, PACK, RUN], f"pre{c}{u}", number)
             for d in range(2):
                 product(pre[:, d].rearrange("p t m -> p (t m)"), d, c, slice(u * HALF, (u + 1) * HALF))
             nc.scalar.activation(h01[c][:, :, :, u, :], pre[:], ACT.Gelu_apprx_tanh)
+
+        for c in range(CHUNKS):
+            pair(c, 0, c)
+        for d in range(2):
+            pre = bank([P, PACK, RUN], f"pre_single{d}", 2 + d)
+            product(pre[:].rearrange("p t m -> p (t m)"), d, 0, slice(HALF, H))
+            nc.scalar.activation(h01[0][:, d, :, 1, :], pre[:], ACT.Gelu_apprx_tanh)
+        pair(1, 1, 4)
         for c in range(CHUNKS):
             pre = bank([P, 2, PACK, RUN], f"pre_last{c}", 5 + c)
             product(pre[:].rearrange("p u t m -> p (u t m)"), 2, c, slice(0, H))
@@ -150,6 +163,9 @@ def tile_picked_statpool_gelu_p_kernel(tc, x_words, x_scales, w1, w2, w3, offs, 
                 w23_bf[:, u, :, :].rearrange("p (c i) j -> p c j i", i=4),
                 w23_raw[u][:].rearrange("p j (c i) -> p c j i", i=4),
             )
+        nc.vector.quantize_mx(
+            out=w23_codes[:].bitcast(FP8X4), scales=w23_scales[:], in_=w23_bf[:].rearrange("p u n j -> p (u n j)")
+        )
 
         def stat(name):
             return [tile([P, PACK, 2, RUN], F32, f"{name}{c}") for c in range(CHUNKS)]
@@ -237,9 +253,6 @@ def tile_picked_statpool_gelu_p_kernel(tc, x_words, x_scales, w1, w2, w3, offs, 
         for c in range(CHUNKS):
             turn(spread[c], diff_sq[c], True)
             turn(spread[c], bend_sq[c], False)
-        nc.vector.quantize_mx(
-            out=w23_codes[:].bitcast(FP8X4), scales=w23_scales[:], in_=w23_bf[:].rearrange("p u n j -> p (u n j)")
-        )
         for c in range(CHUNKS):
             make_mean(c)
         for c in range(CHUNKS):

import math
from contextlib import ExitStack

import concourse.mybir as mybir
from concourse.masks import make_identity

K, T, S, V, H, N = 512, 2048, 768, 256, 512, 128
FLOPS = 2 * K * H * S + 2 * 2 * H * N * V

F32 = mybir.dt.float32
BF16 = mybir.dt.bfloat16
I32 = mybir.dt.int32
U32 = mybir.dt.uint32
U16 = mybir.dt.uint16
U8 = mybir.dt.uint8
FP8X4 = mybir.dt.float8_e4m3fn_x4
FP4X4 = mybir.dt.float4_e2m1fn_x4
ACT = mybir.ActivationFunctionType
ALU = mybir.AluOpType

P = 128
PACK = 4
PIECES = 3
SEG = 128
CHUNKS = V // SEG
QUARTER = H // 4
HALF = H // 2
RUN = HALF // PACK
W1_AHEAD = 1
SQRT_FLOOR = 2.0 ** -110


def tile_picked_statpool_gelu_p_kernel(tc, x_words, x_scales, w1, w2, w3, offs, out):
    nc = tc.nc
    with ExitStack() as ctx:
        sb = ctx.enter_context(tc.tile_pool(name="sb", bufs=1))
        reuse = ctx.enter_context(tc.tile_pool(name="reuse", bufs=1))
        ps = ctx.enter_context(tc.psum_pool(name="ps", bufs=1))

        def tile(shape, dtype, name):
            return sb.tile(shape, dtype, name=name, align_bytes=64)

        def bank(shape, name, number):
            return ps.tile(shape, F32, name=name, tag=f"bank{number}")

        word_table = tile([P, T], U16, "word_table")
        nc.sync.dma_start(word_table[:].bitcast(I32), x_words[0].bitcast(I32))
        offsets = sb.tile([P, S // 16], U16, name="offsets")
        nc.sync.dma_start(offsets[:], offs)

        scale_table = tile([P, T], U8, "scale_table")
        nc.vector.memset(scale_table[:].bitcast(I32), 0)

        zero_in = tile([P, 1], F32, "zero_in")
        zero = tile([P, 1], F32, "zero")
        nc.gpsimd.memset(zero_in[:], 0.0)
        nc.scalar.activation(zero[:], zero_in[:], ACT.Gelu_apprx_tanh)
        floor = tile([P, 1], F32, "floor")
        nc.gpsimd.memset(floor[:], SQRT_FLOOR)
        identity = tile([P, P], F32, "identity")
        make_identity(nc, identity[:])

        raw_bytes = 4 * PACK * QUARTER
        w1_rows = w1.rearrange("(p j) c -> p j c", j=PACK)
        w1_raw = [
            reuse.tile([P, PACK, QUARTER], F32, name=f"w1_raw{q}", align_bytes=64, offset=raw_bytes * q) for q in range(4)
        ]

        def load_w1(q):
            nc.sync.dma_start(w1_raw[q][:], w1_rows[:, :, q * QUARTER : (q + 1) * QUARTER])

        for q in range(W1_AHEAD):
            load_w1(q)
        for r in range(4):
            nc.sync.dma_start(scale_table[r:P:32, :].bitcast(I32), x_scales[0, r:16:4, :].bitcast(I32))
        for q in range(W1_AHEAD, 4):
            load_w1(q)
        w23_raw = [tile([P, PACK, N], F32, f"w23_raw{u}") for u in range(2)]
        for u, w in enumerate((w2, w3)):
            nc.sync.dma_start(w23_raw[u][:], w.rearrange("(p j) n -> p j n", j=PACK))

        picked_words = [tile([P, V], U16, f"picked_words{d}") for d in range(2)]
        picked_words.append(reuse.tile([P, V], U16, name="picked_words2", align_bytes=64, offset=raw_bytes))
        early_scales = tile([P, 2 * V], U8, "early_scales")
        late_scales = reuse.tile([P, V], U8, name="late_scales", align_bytes=64, offset=3 * raw_bytes)
        picked_scales = [early_scales[:, :V], early_scales[:, V:], late_scales[:]]

        def gather_words(d):
            nc.vector.tensor_copy(
                picked_words[d][:], word_table[:].indirect(offsets[:, d * (V // 16) : (d + 1) * (V // 16)])
            )

        w1_bf = [tile([P, PACK, RUN, PACK], BF16, f"w1_bf{u}") for u in range(2)]
        w1_codes = tile([P, H], U32, "w1_codes")
        w1_scales = tile([P, H], U8, "w1_scales")

        def round_w1(q):
            m0 = (q % 2) * (QUARTER // PACK)
            nc.scalar.activation(
                w1_bf[q // 2][:, :, m0 : m0 + QUARTER // PACK, :].rearrange("p t m j -> p m j t"),
                w1_raw[q][:].rearrange("p j (m t) -> p m j t", t=PACK),
                ACT.Identity,
                bias=zero[:],
            )

        def quantise_w1(u):
            cols = slice(u * HALF, (u + 1) * HALF)
            nc.vector.quantize_mx(
                out=w1_codes[:, cols].bitcast(FP8X4),
                scales=w1_scales[:, cols],
                in_=w1_bf[u][:].rearrange("p t m j -> p (t m j)"),
            )

        gather_words(0)
        gather_words(1)
        nc.vector.tensor_copy(early_scales[:], scale_table[:].indirect(offsets[:, : 2 * V // 16]))
        round_w1(0)
        round_w1(1)
        quantise_w1(0)
        gather_words(2)
        round_w1(2)
        round_w1(3)
        quantise_w1(1)
        nc.vector.tensor_copy(late_scales[:], scale_table[:].indirect(offsets[:, 2 * V // 16 :]))

        h01 = [tile([P, 2, PACK, 2, RUN], F32, f"h01_{c}") for c in range(CHUNKS)]
        h2 = [tile([P, PACK, 2, RUN], F32, f"h2_{c}") for c in range(CHUNKS)]

        def product(dst, d, c, cols):
            nc.tensor.matmul_mx(
                out=dst,
                lhsT=picked_words[d][:, c * SEG : (c + 1) * SEG].bitcast(FP4X4),
                lhsT_scale=picked_scales[d][:, c * SEG : (c + 1) * SEG],
                rhs=w1_codes[:, cols].bitcast(FP8X4),
                rhs_scale=w1_scales[:, cols],
                start=True,
                stop=True,
            )

        def pair(c, u, number):
            pre = bank([P, 2, PACK, RUN], f"pre{c}{u}", number)
            for d in range(2):
                product(pre[:, d].rearrange("p t m -> p (t m)"), d, c, slice(u * HALF, (u + 1) * HALF))
            nc.scalar.activation(h01[c][:, :, :, u, :], pre[:], ACT.Gelu_apprx_tanh)

        for c in range(CHUNKS):
            pair(c, 0, c)
        for d in range(2):
            pre = bank([P, PACK, RUN], f"pre_single{d}", 2 + d)
            product(pre[:].rearrange("p t m -> p (t m)"), d, 0, slice(HALF, H))
            nc.scalar.activation(h01[0][:, d, :, 1, :], pre[:], ACT.Gelu_apprx_tanh)
        pair(1, 1, 4)
        for c in range(CHUNKS):
            pre = bank([P, 2, PACK, RUN], f"pre_last{c}", 5 + c)
            product(pre[:].rearrange("p u t m -> p (u t m)"), 2, c, slice(0, H))
            nc.scalar.activation(h2[c][:].rearrange("p t u m -> p u t m"), pre[:], ACT.Gelu_apprx_tanh)

        w23_bf = tile([P, 2, N, PACK], BF16, "w23_bf")
        w23_codes = tile([P, 2 * N], U32, "w23_codes")
        w23_scales = tile([P, 2 * N], U8, "w23_scales")
        for u in range(2):
            nc.vector.tensor_copy(
                w23_bf[:, u, :, :].rearrange("p (c i) j -> p c j i", i=4),
                w23_raw[u][:].rearrange("p j (c i) -> p c j i", i=4),
            )
        nc.vector.quantize_mx(
            out=w23_codes[:].bitcast(FP8X4), scales=w23_scales[:], in_=w23_bf[:].rearrange("p u n j -> p (u n j)")
        )

        def stat(name):
            return [tile([P, PACK, 2, RUN], F32, f"{name}{c}") for c in range(CHUNKS)]

        pair_sum, pair_diff, bend, diff_sq, bend_sq = (
            stat(name) for name in ("pair_sum", "pair_diff", "bend", "diff_sq", "bend_sq")
        )
        stat_bf = [[tile([P, SEG, PACK], BF16, f"stat_bf{k}{c}") for c in range(CHUNKS)] for k in range(2)]
        stat_codes = [tile([P, V], U32, f"stat_codes{k}") for k in range(2)]
        stat_scales = [tile([P, V], U8, f"stat_scales{k}") for k in range(2)]

        def flat(t):
            return t[:].rearrange("p t u m -> p (t u m)")

        def make_pair(c, u):
            nc.vector.tensor_tensor(pair_sum[c][:, :, u, :], h01[c][:, 0, :, u, :], h01[c][:, 1, :, u, :], ALU.add)
            nc.vector.tensor_tensor(pair_diff[c][:, :, u, :], h01[c][:, 0, :, u, :], h01[c][:, 1, :, u, :], ALU.subtract)

        def make_bend(c):
            nc.vector.scalar_tensor_tensor(flat(bend[c]), flat(h2[c]), -2.0, flat(pair_sum[c]), ALU.mult, ALU.add)

        def square_diff(c):
            nc.scalar.activation(flat(diff_sq[c]), flat(pair_diff[c]), ACT.Square, scale=math.sqrt(3.0))

        def square_bend(c):
            nc.vector.tensor_tensor(flat(bend_sq[c]), flat(bend[c]), flat(bend[c]), ALU.mult)

        def turn(dst, src, first):
            for t in range(PACK):
                nc.tensor.matmul(
                    dst[:, t, :],
                    flat(src)[:, t * P : (t + 1) * P],
                    identity[:],
                    start=first and t == 0,
                    stop=not first and t == PACK - 1,
                    is_transpose=True,
                )

        total = [bank([P, PACK, SEG], f"total{c}", (7, 0)[c]) for c in range(CHUNKS)]
        spread = [bank([P, PACK, SEG], f"spread{c}", 1 + c) for c in range(CHUNKS)]

        def make_mean(c):
            nc.vector.tensor_scalar_mul(stat_bf[0][c][:], total[c][:].rearrange("p t v -> p v t"), 1.0 / 3.0)

        def make_dev(c):
            nc.scalar.activation(
                stat_bf[1][c][:], spread[c][:].rearrange("p t v -> p v t"), ACT.Sqrt, scale=1.0 / 18.0, bias=floor[:]
            )

        def quantise(k, c):
            cols = slice(c * SEG, (c + 1) * SEG)
            nc.vector.quantize_mx(
                out=stat_codes[k][:, cols].bitcast(FP8X4),
                scales=stat_scales[k][:, cols],
                in_=stat_bf[k][c][:].rearrange("p v t -> p (v t)"),
            )

        def finish(c):
            acc = bank([P, SEG], f"acc{c}", 3 + c)
            cols = slice(c * SEG, (c + 1) * SEG)
            for k in range(2):
                nc.tensor.matmul_mx(
                    out=acc[:],
                    lhsT=w23_codes[:, k * N : (k + 1) * N].bitcast(FP8X4),
                    lhsT_scale=w23_scales[:, k * N : (k + 1) * N],
                    rhs=stat_codes[k][:, cols].bitcast(FP8X4),
                    rhs_scale=stat_scales[k][:, cols],
                    start=(k == 0),
                    stop=(k == 1),
                )
            result = tile([P, SEG], F32, f"result{c}")
            nc.scalar.copy(result[:], acc[:])
            nc.sync.dma_start(out[:, cols], result[:])

        for c, u in ((0, 0), (1, 0), (0, 1), (1, 1)):
            make_pair(c, u)
        for c in range(CHUNKS):
            make_bend(c)
        for c in range(CHUNKS):
            square_diff(c)
            turn(total[c], pair_sum[c], True)
            turn(total[c], h2[c], False)
        for c in range(CHUNKS):
            square_bend(c)
        for c in range(CHUNKS):
            turn(spread[c], diff_sq[c], True)
            turn(spread[c], bend_sq[c], False)
        for c in range(CHUNKS):
            make_mean(c)
        for c in range(CHUNKS):
            make_dev(c)
            quantise(0, c)
        for c in range(CHUNKS):
            quantise(1, c)
        for c in range(CHUNKS):
            finish(c)
